import numpy as np
CORES = [21,109,149,237,277,365,405,493,150,406]
N = 10
TK = 128
D = 128 * N
EPS = 0.01
def setup_inputs(rng):
    x = rng.standard_normal((N, 128, TK), dtype=np.float32) * (0.5 + np.abs(rng.standard_normal((1, 1, TK), dtype=np.float32))) + rng.standard_normal((1, 1, TK), dtype=np.float32)
    return {"x": x, "dy": rng.standard_normal((N, 128, TK), dtype=np.float32) + 0.5 * x + rng.standard_normal((1, 1, TK), dtype=np.float32)}
def setup_inputs_big(rng):
    d = setup_inputs(rng)
    for k in ("x", "dy"): d[k] = (d[k].astype(np.float32) * 1024.0).astype(d[k].dtype)
    return d
def setup_inputs_small(rng):
    d = setup_inputs(rng)
    for k in ("x", "dy"): d[k] = (d[k].astype(np.float32) * (1 / 1024.0)).astype(d[k].dtype)
    return d
def setup_inputs_apart(rng):
    d = setup_inputs(rng)
    f = (10.0 ** rng.permutation(np.linspace(-1.5, 1.5, N))).astype(np.float32).reshape(N, 1, 1)
    for k in ("x",): d[k] = (d[k].astype(np.float32) * f).astype(d[k].dtype)
    return d
def setup_inputs_mixed(rng):
    d = setup_inputs(rng)
    f = (10.0 ** rng.uniform(-3, 3, (1, 1, TK))).astype(np.float32); shape = rng.integers(3, size=(1, 1, TK))
    for k in ("x", "dy"):
        x = d[k].astype(np.float32)
        m = x.mean(axis=(0, 1), keepdims=True); level = m + np.sign(x - m) * np.abs(x - m).mean(axis=(0, 1), keepdims=True) * rng.uniform(0.9, 1.1, x.shape).astype(np.float32)
        other = x * np.where(rng.random(x.shape) < 0.5, 0.1, 1.0).astype(np.float32)
        d[k] = (np.where(shape == 1, level, np.where(shape == 2, other, x)) * f).astype(d[k].dtype)
    return d
def setup_inputs_offset(rng):
    d = setup_inputs(rng)
    x = d["x"]; spread = x.std(axis=(0, 1), keepdims=True)
    d["x"] = (x + spread * rng.uniform(16, 48, (1, 1, TK)) * rng.choice([-1.0, 1.0], (1, 1, TK))).astype(np.float32)
    return d
def reference(x, dy):
    X, DY = x.astype(np.float64), dy.astype(np.float64)
    mu = X.sum(axis=(0, 1)) / D
    rs = 1.0 / np.sqrt(((X - mu) ** 2).sum(axis=(0, 1)) / D + EPS)
    n = (X - mu) * rs
    a = DY.sum(axis=(0, 1)) / D; c = (DY * n).sum(axis=(0, 1)) / D
    return {"dx": (rs * (DY - a - n * c)).astype(np.float32)}

@@ -1,0 +1,264 @@
+from concourse.bass import DstId, RemoteDMATransfer
+from concourse.mybir import AluOpType, AxisListType, ActivationFunctionType
+
+NR = 10
+TK = 128
+D = 128 * NR
+EPS = 0.01
+NSTAT = 4
+HOP1_ENGINES = 4
+
+SCRATCH = {
+    "x_sb": ("sbuf", [128, 128], "float32"),
+    "dy_sb": ("sbuf", [128, 128], "float32"),
+    "ident": ("sbuf", [128, 128], "float32"),
+    "k11": ("sbuf", [128, 12], "float32"),
+    "xT": ("sbuf", [128, 128], "float32"),
+    "dyT": ("sbuf", [128, 128], "float32"),
+    "xc": ("sbuf", [128, 128], "float32"),
+    "pr": ("sbuf", [128, 128], "float32"),
+    "junk": ("sbuf", [128, 128], "float32"),
+    "stat": ("sbuf", [128, NSTAT], "float32"),
+    "col": ("sbuf", [128, 16], "float32"),
+    "G": ("sbuf", [128, 128 * NSTAT], "float32"),
+    "j10": ("sbuf", [128, 12], "float32"),
+    "dl": ("sbuf", [128, 12], "float32"),
+    "dA": ("sbuf", [128, 12], "float32"),
+    "w": ("sbuf", [128, 128], "float32"),
+    "u": ("sbuf", [128, 128], "float32"),
+    "t3": ("sbuf", [128, 128], "float32"),
+    "dsd": ("sbuf", [128, 128], "float32"),
+    "dx_sb": ("sbuf", [128, 128], "float32"),
+    "hub": ("dram", [3, 128, NSTAT], "float32"),
+    "gd": ("dram", [NR, 128, NSTAT], "float32"),
+    "xT_ps": ("psum", [128, 512], "float32"),
+    "dyT_ps": ("psum", [128, 512], "float32"),
+    "tm_ps": ("psum", [128, 512], "float32"),
+    "tM_ps": ("psum", [128, 512], "float32"),
+    "tA_ps": ("psum", [128, 512], "float32"),
+    "tC_ps": ("psum", [128, 512], "float32"),
+    "dx_ps": ("psum", [128, 512], "float32"),
+}
+NSEM = 48
+SEMAPHORES = ["harr", "arr", "lsem"] + ["s%d" % k for k in range(NSEM)]
+
+_CACHE = {}
+
+
+def _plan(T, topo):
+    if "hubs" in _CACHE:
+        return _CACHE["hubs"]
+    ranks = list(T.cores)
+    hosts = sorted({topo.host(c) for c in ranks})
+    kinds = [[c] for c in ranks]
+    merged = True
+    while merged:
+        merged = False
+        for i in range(len(kinds)):
+            for j in range(i + 1, len(kinds)):
+                if any(topo.may_write(a, b) and topo.may_write(b, a) for a in kinds[i] for b in kinds[j]):
+                    kinds[i] = kinds[i] + kinds[j]
+                    del kinds[j]
+                    merged = True
+                    break
+            if merged:
+                break
+
+    def cabled(h):
+        for h2 in hosts:
+            if topo.rack(h2) != topo.rack(h) and any(
+                    topo.may_write(a, b) for a in ranks if topo.host(a) == h for b in ranks if topo.host(b) == h2):
+                return h2
+        return None
+
+    hubs = []
+    for kind in kinds:
+        for h in hosts:
+            here = [c for c in kind if topo.host(c) == h]
+            srcs = here + [c for c in kind if topo.host(c) == cabled(h)]
+            dsts = [c for c in ranks if topo.rack(topo.host(c)) == topo.rack(h)]
+            cand = [c for c in range(max(ranks) + 128)
+                    if topo.host(c) == h and topo.chip(c) == topo.chip(here[0]) and c not in ranks
+                    and topo.die(c) == topo.die(here[0])
+                    and all(topo.may_write(c, d) for d in dsts) and all(topo.may_write(s, c) for s in srcs)]
+            hubs.append((cand[0], srcs, dsts))
+    for d in ranks:
+        got = sorted(s for (_, srcs, dsts) in hubs if d in dsts for s in srcs)
+        assert got == sorted(ranks)
+    _CACHE["hubs"] = hubs
+    return hubs
+
+
+def _engines(topo, src, dsts):
+    m = topo.mask(src, dsts[0])
+    for d in dsts[1:]:
+        m &= topo.mask(src, d)
+    return [e for e in range(16) if (m >> e) & 1]
+
+
+def _bits(es):
+    m = 0
+    for e in es:
+        m |= 1 << e
+    return m
+
+
+def _dst(topo, d, src):
+    rid, pid = topo.addr(d, src)
+    return DstId(rid=rid, pnc=pid)
+
+
+def _hub_program(g, core, T, topo, srcs, dsts):
+    g.wait_ge(T.sem.harr, HOP1_ENGINES * len(srcs))
+    es = _engines(topo, core, dsts)[0::2]
+    trs = []
+    for i, s in enumerate(srcs):
+        r = T.rank_of(s)
+        trs.append(RemoteDMATransfer(dst_ids=[_dst(topo, d, core) for d in dsts], dma_engine_mask=_bits([es[i]]),
+                                     remote_sem=T.sem.arr, srcs=[T.hub[i]], dsts=[T.gd[r] for _ in dsts]))
+    g.remote_dma_fused(trs, local_sem=T.sem.lsem)
+    g.wait_ge(T.sem.lsem, len(srcs))
+
+
+def rank_program(g, core, T, topo):
+    hubs = _plan(T, topo)
+    for (h, srcs, dsts) in hubs:
+        if h == core:
+            _hub_program(g, core, T, topo, srcs, dsts)
+            return
+    if T.rank_of(core) is None:
+        return
+
+    V, A, P, S = g.vector, g.scalar, g.tensor, g.sync
+    MUL, ADD, SUB = AluOpType.mult, AluOpType.add, AluOpType.subtract
+    F = ActivationFunctionType
+    n = [0]
+
+    def sem():
+        n[0] += 1
+        return T.sem["s%d" % (n[0] - 1)]
+
+    def col(k):
+        return T.col[:, k:k + 1]
+
+    S1, POSMU, NEGMU, V1, SSD, VV, RV, RVD, NEGA, SDA, CS, Q2 = [col(k) for k in range(12)]
+
+    s_x, s_dy = sem(), sem()
+    S.dma_start(T.x_sb[:], T.x[:]).then_inc(s_x, 16)
+    A.dma_start(T.dy_sb[:], T.dy[:]).then_inc(s_dy, 16)
+    s_one, s_k1, s_id, s_k11 = sem(), sem(), sem(), sem()
+    V.memset(T.ident[:], 1.0).then_inc(s_one, 1)
+    V.memset(T.k11[0:NR, 0:NR + 1], 1.0).then_inc(s_k1, 1)
+    g.wait_ge(s_one, 1)
+    g.affine_select(T.ident[:], T.ident[:], [[-1, 128]], AluOpType.is_equal, 0.0, 0, 1).then_inc(s_id, 1)
+    g.wait_ge(s_k1, 1)
+    g.affine_select(T.k11[0:NR, 0:NR], T.k11[0:NR, 0:NR], [[-1, NR]], AluOpType.is_equal, 0.0, 0, 1).then_inc(s_k11, 1)
+
+    s_xT, s_dyT = sem(), sem()
+    P.wait_ge(s_id, 1)
+    P.wait_ge(s_x, 16)
+    P.transpose(T.xT_ps[:, 0:128], T.x_sb[:], T.ident[:]).then_inc(s_xT, 1)
+    P.wait_ge(s_dy, 16)
+    P.transpose(T.dyT_ps[:, 0:128], T.dy_sb[:], T.ident[:]).then_inc(s_dyT, 1)
+
+    s_s1, s_m, s_xc, s_pr, s_c, s_M, s_A = sem(), sem(), sem(), sem(), sem(), sem(), sem()
+    A.wait_ge(s_xT, 1)
+    A.activation(T.xT[:], T.xT_ps[:, 0:128], F.Identity, accum_out=S1).then_inc(s_s1, 1)
+    V.wait_ge(s_s1, 1)
+    V.tensor_scalar(T.stat[:, 0:1], S1, -1.0 / 128.0, None, MUL).then_inc(s_m, 1)
+    V.wait_ge(s_m, 1)
+    V.tensor_scalar(T.xc[:], T.xT[:], T.stat[:, 0:1], None, ADD).then_inc(s_xc, 1)
+    A.wait_ge(s_m, 1)
+    A.activation(T.junk[:], T.xT[:], F.Square, bias=T.stat[:, 0:1], accum_out=T.stat[:, 2:3]).then_inc(s_M, 1)
+    V.wait_ge(s_xc, 1)
+    V.wait_ge(s_dyT, 1)
+    V.tensor_tensor(T.pr[:], T.dyT_ps[:, 0:128], T.xc[:], MUL).then_inc(s_pr, 1)
+    V.wait_ge(s_pr, 1)
+    V.tensor_reduce(T.stat[:, 3:4], T.pr[:], AxisListType.X, ADD).then_inc(s_c, 1)
+    A.wait_ge(s_pr, 1)
+    A.activation(T.dyT[:], T.dyT_ps[:, 0:128], F.Identity, accum_out=T.stat[:, 1:2]).then_inc(s_A, 1)
+
+    mine = [(h, srcs.index(core)) for (h, srcs, _) in hubs if core in srcs]
+    far = [e for (h, _) in mine for e in _engines(topo, core, [h])]
+    narrow = [e for e in range(16) if far.count(e) == len(mine)]
+    used, trs = [], []
+    for (h, slot) in sorted(mine, key=lambda t: len(_engines(topo, core, [t[0]]))):
+        es = _engines(topo, core, [h])
+        wide = [e for e in es if e not in narrow and e not in used]
+        pick = (wide if len(wide) >= 2 * HOP1_ENGINES else [e for e in es if e not in used])[0::2][0:HOP1_ENGINES]
+        used += pick
+        trs.append(RemoteDMATransfer(dst_ids=[_dst(topo, h, core)], dma_engine_mask=_bits(pick),
+                                     remote_sem=T.sem.harr, srcs=[T.stat[:]], dsts=[T.hub[slot]]))
+    for s in (s_m, s_A, s_M, s_c):
+        g.wait_ge(s, 1)
+    g.remote_dma_fused(trs, local_sem=T.sem.lsem)
+
+    s_G = sem()
+    S.wait_ge(T.sem.arr, NR)
+    S.dma_start(T.G[0:NR, :], T.gd[:]).then_inc(s_G, 16)
+
+    W = 128 * NSTAT
+    s_tm, s_tM, s_tA, s_tC = sem(), sem(), sem(), sem()
+    P.wait_ge(s_k11, 1)
+    P.wait_ge(s_G, 16)
+    P.matmul(T.tm_ps[:, 0:NR + 1], T.G[0:NR, 0:W:NSTAT], T.k11[0:NR, 0:NR + 1], True, True).then_inc(s_tm, 1)
+    P.matmul(T.tM_ps[:, 0:1], T.G[0:NR, 2:W:NSTAT], T.k11[0:NR, NR:NR + 1], True, True).then_inc(s_tM, 1)
+    P.matmul(T.tA_ps[:, 0:NR + 1], T.G[0:NR, 1:W:NSTAT], T.k11[0:NR, 0:NR + 1], True, True).then_inc(s_tA, 1)
+    P.matmul(T.tC_ps[:, 0:1], T.G[0:NR, 3:W:NSTAT], T.k11[0:NR, NR:NR + 1], True, True).then_inc(s_tC, 1)
+
+    s_pm, s_v1, s_nm, s_ssd, s_v = sem(), sem(), sem(), sem(), sem()
+    V.wait_ge(s_tm, 1)
+    V.tensor_scalar(POSMU, T.tm_ps[:, NR:NR + 1], -1.0 / NR, None, MUL).then_inc(s_pm, 1)
+    A.wait_ge(s_pm, 1)
+    A.activation(T.j10[:, 0:NR], T.tm_ps[:, 0:NR], F.Square, bias=POSMU, accum_out=SSD).then_inc(s_ssd, 1)
+    V.wait_ge(s_tM, 1)
+    V.tensor_scalar(V1, T.tM_ps[:, 0:1], 1.0 / D, EPS, MUL, ADD).then_inc(s_v1, 1)
+    V.wait_ge(s_pm, 1)
+    V.tensor_scalar(NEGMU, POSMU, -1.0, None, MUL).then_inc(s_nm, 1)
+    V.wait_ge(s_ssd, 1)
+    V.wait_ge(s_v1, 1)
+    V.tensor_scalar(VV, SSD, 128.0 / D, V1, MUL, ADD).then_inc(s_v, 1)
+
+    s_dsd = sem()
+    A.wait_ge(s_v, 1)
+    A.wait_ge(s_id, 1)
+    A.activation(T.dsd[:], T.ident[:], F.Sqrt, scale=VV).then_inc(s_dsd, 1)
+
+    s_rv, s_dl, s_dA, s_na, s_sdA, s_rvD, s_w, s_Cs, s_q2, s_u, s_t3 = [sem() for _ in range(11)]
+    V.wait_ge(s_v, 1)
+    V.reciprocal(RV, VV).then_inc(s_rv, 1)
+    V.tensor_scalar(T.dl[:, 0:NR], T.tm_ps[:, 0:NR], POSMU, None, ADD).then_inc(s_dl, 1)
+    V.wait_ge(s_tA, 1)
+    V.tensor_scalar(NEGA, T.tA_ps[:, NR:NR + 1], -1.0 / D, None, MUL).then_inc(s_na, 1)
+    V.wait_ge(s_dl, 1)
+    V.tensor_tensor(T.dA[:, 0:NR], T.dl[:, 0:NR], T.tA_ps[:, 0:NR], MUL).then_inc(s_dA, 1)
+    V.wait_ge(s_dA, 1)
+    V.tensor_reduce(SDA, T.dA[:, 0:NR], AxisListType.X, ADD).then_inc(s_sdA, 1)
+    V.wait_ge(s_rv, 1)
+    V.tensor_scalar(RVD, RV, 1.0 / D, None, MUL).then_inc(s_rvD, 1)
+    V.wait_ge(s_sdA, 1)
+    V.wait_ge(s_tC, 1)
+    V.tensor_scalar(CS, T.tC_ps[:, 0:1], SDA, None, SUB).then_inc(s_Cs, 1)
+    V.wait_ge(s_Cs, 1)
+    V.wait_ge(s_rvD, 1)
+    V.tensor_scalar(Q2, CS, RV, RVD, MUL, MUL).then_inc(s_q2, 1)
+    V.wait_ge(s_na, 1)
+    V.wait_ge(s_A, 1)
+    V.tensor_scalar(T.w[:], T.dyT[:], NEGA, RV, ADD, MUL).then_inc(s_w, 1)
+    V.wait_ge(s_q2, 1)
+    V.wait_ge(s_nm, 1)
+    V.tensor_scalar(T.u[:], T.xT[:], NEGMU, Q2, ADD, MUL).then_inc(s_u, 1)
+    V.wait_ge(s_u, 1)
+    V.wait_ge(s_w, 1)
+    V.tensor_tensor(T.t3[:], T.w[:], T.u[:], SUB).then_inc(s_t3, 1)
+
+    s_dx, s_o, s_st = sem(), sem(), sem()
+    P.wait_ge(s_t3, 1)
+    P.wait_ge(s_dsd, 1)
+    P.matmul(T.dx_ps[:, 0:128], T.t3[:], T.dsd[:], True, True).then_inc(s_dx, 1)
+    V.wait_ge(s_dx, 1)
+    V.tensor_copy(T.dx_sb[:], T.dx_ps[:, 0:128]).then_inc(s_o, 1)
+    S.wait_ge(s_o, 1)
+    S.dma_start(T.dx[:], T.dx_sb[:]).then_inc(s_st, 16)
+    S.wait_ge(s_st, 16)
+    g.wait_ge(T.sem.lsem, HOP1_ENGINES * len(trs))

@@ -5,22 +5,26 @@ NR = 10
 TK = 128
 D = 128 * NR
 EPS = 0.01
-NSTAT = 4
+NS2 = 3
 HOP1_ENGINES = 4
+HUB_ENGINES = 1
 
 SCRATCH = {
     "x_sb": ("sbuf", [128, 128], "float32"),
     "dy_sb": ("sbuf", [128, 128], "float32"),
     "ident": ("sbuf", [128, 128], "float32"),
+    "onec": ("sbuf", [128, 4], "float32"),
     "k11": ("sbuf", [128, 12], "float32"),
     "xT": ("sbuf", [128, 128], "float32"),
     "dyT": ("sbuf", [128, 128], "float32"),
     "xc": ("sbuf", [128, 128], "float32"),
     "pr": ("sbuf", [128, 128], "float32"),
     "junk": ("sbuf", [128, 128], "float32"),
-    "stat": ("sbuf", [128, NSTAT], "float32"),
+    "stat1": ("sbuf", [128, 1], "float32"),
+    "stat2": ("sbuf", [128, NS2], "float32"),
     "col": ("sbuf", [128, 16], "float32"),
-    "G": ("sbuf", [128, 128 * NSTAT], "float32"),
+    "G1": ("sbuf", [128, 128], "float32"),
+    "G2": ("sbuf", [128, 128 * NS2], "float32"),
     "j10": ("sbuf", [128, 12], "float32"),
     "dl": ("sbuf", [128, 12], "float32"),
     "dA": ("sbuf", [128, 12], "float32"),
@@ -29,8 +33,11 @@ SCRATCH = {
     "t3": ("sbuf", [128, 128], "float32"),
     "dsd": ("sbuf", [128, 128], "float32"),
     "dx_sb": ("sbuf", [128, 128], "float32"),
-    "hub": ("dram", [3, 128, NSTAT], "float32"),
-    "gd": ("dram", [NR, 128, NSTAT], "float32"),
+    "hub1": ("dram", [3, 128, 1], "float32"),
+    "hub2": ("dram", [3, 128, NS2], "float32"),
+    "gd1": ("dram", [NR, 128, 1], "float32"),
+    "gd2": ("dram", [NR, 128, NS2], "float32"),
+    "s1_ps": ("psum", [128, 512], "float32"),
     "xT_ps": ("psum", [128, 512], "float32"),
     "dyT_ps": ("psum", [128, 512], "float32"),
     "tm_ps": ("psum", [128, 512], "float32"),
@@ -40,7 +47,7 @@ SCRATCH = {
     "dx_ps": ("psum", [128, 512], "float32"),
 }
 NSEM = 48
-SEMAPHORES = ["harr", "arr", "lsem"] + ["s%d" % k for k in range(NSEM)]
+SEMAPHORES = ["harr1", "harr2", "arr1", "arr2", "lsem"] + ["s%d" % k for k in range(NSEM)]
 
 _CACHE = {}
 
@@ -96,6 +103,10 @@ def _engines(topo, src, dsts):
     return [e for e in range(16) if (m >> e) & 1]
 
 
+def _spread(es):
+    return es[0::2] + es[1::2]
+
+
 def _bits(es):
     m = 0
     for e in es:
@@ -109,15 +120,19 @@ def _dst(topo, d, src):
 
 
 def _hub_program(g, core, T, topo, srcs, dsts):
-    g.wait_ge(T.sem.harr, HOP1_ENGINES * len(srcs))
-    es = _engines(topo, core, dsts)[0::2]
-    trs = []
-    for i, s in enumerate(srcs):
-        r = T.rank_of(s)
-        trs.append(RemoteDMATransfer(dst_ids=[_dst(topo, d, core) for d in dsts], dma_engine_mask=_bits([es[i]]),
-                                     remote_sem=T.sem.arr, srcs=[T.hub[i]], dsts=[T.gd[r] for _ in dsts]))
-    g.remote_dma_fused(trs, local_sem=T.sem.lsem)
-    g.wait_ge(T.sem.lsem, len(srcs))
+    es = _spread(_engines(topo, core, dsts))
+    k = HUB_ENGINES
+    for (landed, slots, out, arrived) in ((T.sem.harr1, T.hub1, T.gd1, T.sem.arr1),
+                                          (T.sem.harr2, T.hub2, T.gd2, T.sem.arr2)):
+        g.wait_ge(landed, HOP1_ENGINES * len(srcs))
+        trs = []
+        for i, s in enumerate(srcs):
+            r = T.rank_of(s)
+            trs.append(RemoteDMATransfer(dst_ids=[_dst(topo, d, core) for d in dsts],
+                                         dma_engine_mask=_bits(es[i * k:(i + 1) * k]),
+                                         remote_sem=arrived, srcs=[slots[i]], dsts=[out[r] for _ in dsts]))
+        g.remote_dma_fused(trs, local_sem=T.sem.lsem)
+    g.wait_ge(T.sem.lsem, 2 * k * len(srcs))
 
 
 def rank_program(g, core, T, topo):
@@ -141,12 +156,14 @@ def rank_program(g, core, T, topo):
     def col(k):
         return T.col[:, k:k + 1]
 
-    S1, POSMU, NEGMU, V1, SSD, VV, RV, RVD, NEGA, SDA, CS, Q2 = [col(k) for k in range(12)]
+    POSMU, NEGMU, V1, SSD, VV, RV, RVD, NEGA, SDA, CS, Q2 = [col(k) for k in range(11)]
+    M_R = T.stat1[:, 0:1]
 
     s_x, s_dy = sem(), sem()
     S.dma_start(T.x_sb[:], T.x[:]).then_inc(s_x, 16)
     A.dma_start(T.dy_sb[:], T.dy[:]).then_inc(s_dy, 16)
-    s_one, s_k1, s_id, s_k11 = sem(), sem(), sem(), sem()
+    s_oc, s_one, s_k1, s_id, s_k11 = sem(), sem(), sem(), sem(), sem()
+    V.memset(T.onec[:, 0:1], 1.0).then_inc(s_oc, 1)
     V.memset(T.ident[:], 1.0).then_inc(s_one, 1)
     V.memset(T.k11[0:NR, 0:NR + 1], 1.0).then_inc(s_k1, 1)
     g.wait_ge(s_one, 1)
@@ -154,67 +171,79 @@ def rank_program(g, core, T, topo):
     g.wait_ge(s_k1, 1)
     g.affine_select(T.k11[0:NR, 0:NR], T.k11[0:NR, 0:NR], [[-1, NR]], AluOpType.is_equal, 0.0, 0, 1).then_inc(s_k11, 1)
 
-    s_xT, s_dyT = sem(), sem()
-    P.wait_ge(s_id, 1)
+    s_s1, s_xT, s_dyT = sem(), sem(), sem()
+    P.wait_ge(s_oc, 1)
     P.wait_ge(s_x, 16)
+    P.matmul(T.s1_ps[:, 0:1], T.x_sb[:], T.onec[:, 0:1], True, True).then_inc(s_s1, 1)
+    P.wait_ge(s_id, 1)
     P.transpose(T.xT_ps[:, 0:128], T.x_sb[:], T.ident[:]).then_inc(s_xT, 1)
     P.wait_ge(s_dy, 16)
     P.transpose(T.dyT_ps[:, 0:128], T.dy_sb[:], T.ident[:]).then_inc(s_dyT, 1)
 
-    s_s1, s_m, s_xc, s_pr, s_c, s_M, s_A = sem(), sem(), sem(), sem(), sem(), sem(), sem()
-    A.wait_ge(s_xT, 1)
-    A.activation(T.xT[:], T.xT_ps[:, 0:128], F.Identity, accum_out=S1).then_inc(s_s1, 1)
+    s_m, s_xs, s_xc, s_pr, s_c, s_M, s_A = sem(), sem(), sem(), sem(), sem(), sem(), sem()
     V.wait_ge(s_s1, 1)
-    V.tensor_scalar(T.stat[:, 0:1], S1, -1.0 / 128.0, None, MUL).then_inc(s_m, 1)
+    V.tensor_scalar(M_R, T.s1_ps[:, 0:1], -1.0 / 128.0, None, MUL).then_inc(s_m, 1)
+    A.wait_ge(s_xT, 1)
+    A.activation(T.xT[:], T.xT_ps[:, 0:128], F.Identity).then_inc(s_xs, 1)
     V.wait_ge(s_m, 1)
-    V.tensor_scalar(T.xc[:], T.xT[:], T.stat[:, 0:1], None, ADD).then_inc(s_xc, 1)
+    V.wait_ge(s_xs, 1)
+    V.tensor_scalar(T.xc[:], T.xT[:], M_R, None, ADD).then_inc(s_xc, 1)
     A.wait_ge(s_m, 1)
-    A.activation(T.junk[:], T.xT[:], F.Square, bias=T.stat[:, 0:1], accum_out=T.stat[:, 2:3]).then_inc(s_M, 1)
+    A.wait_ge(s_xs, 1)
+    A.activation(T.junk[:], T.xT[:], F.Square, bias=M_R, accum_out=T.stat2[:, 1:2]).then_inc(s_M, 1)
     V.wait_ge(s_xc, 1)
     V.wait_ge(s_dyT, 1)
     V.tensor_tensor(T.pr[:], T.dyT_ps[:, 0:128], T.xc[:], MUL).then_inc(s_pr, 1)
     V.wait_ge(s_pr, 1)
-    V.tensor_reduce(T.stat[:, 3:4], T.pr[:], AxisListType.X, ADD).then_inc(s_c, 1)
+    V.tensor_reduce(T.stat2[:, 2:3], T.pr[:], AxisListType.X, ADD).then_inc(s_c, 1)
     A.wait_ge(s_pr, 1)
-    A.activation(T.dyT[:], T.dyT_ps[:, 0:128], F.Identity, accum_out=T.stat[:, 1:2]).then_inc(s_A, 1)
+    A.activation(T.dyT[:], T.dyT_ps[:, 0:128], F.Identity, accum_out=T.stat2[:, 0:1]).then_inc(s_A, 1)
 
     mine = [(h, srcs.index(core)) for (h, srcs, _) in hubs if core in srcs]
     far = [e for (h, _) in mine for e in _engines(topo, core, [h])]
     narrow = [e for e in range(16) if far.count(e) == len(mine)]
-    used, trs = [], []
+    used, ways = [], []
     for (h, slot) in sorted(mine, key=lambda t: len(_engines(topo, core, [t[0]]))):
         es = _engines(topo, core, [h])
         wide = [e for e in es if e not in narrow and e not in used]
-        pick = (wide if len(wide) >= 2 * HOP1_ENGINES else [e for e in es if e not in used])[0::2][0:HOP1_ENGINES]
+        pick = _spread(wide if len(wide) >= HOP1_ENGINES else [e for e in es if e not in used])[0:HOP1_ENGINES]
         used += pick
-        trs.append(RemoteDMATransfer(dst_ids=[_dst(topo, h, core)], dma_engine_mask=_bits(pick),
-                                     remote_sem=T.sem.harr, srcs=[T.stat[:]], dsts=[T.hub[slot]]))
-    for s in (s_m, s_A, s_M, s_c):
+        ways.append((h, slot, _bits(pick)))
+    g.wait_ge(s_m, 1)
+    g.remote_dma_fused([RemoteDMATransfer(dst_ids=[_dst(topo, h, core)], dma_engine_mask=m, remote_sem=T.sem.harr1,
+                                          srcs=[T.stat1[:]], dsts=[T.hub1[slot]]) for (h, slot, m) in ways],
+                       local_sem=T.sem.lsem)
+    for s in (s_A, s_M, s_c):
         g.wait_ge(s, 1)
-    g.remote_dma_fused(trs, local_sem=T.sem.lsem)
+    g.remote_dma_fused([RemoteDMATransfer(dst_ids=[_dst(topo, h, core)], dma_engine_mask=m, remote_sem=T.sem.harr2,
+                                          srcs=[T.stat2[:]], dsts=[T.hub2[slot]]) for (h, slot, m) in ways],
+                       local_sem=T.sem.lsem)
 
-    s_G = sem()
-    S.wait_ge(T.sem.arr, NR)
-    S.dma_start(T.G[0:NR, :], T.gd[:]).then_inc(s_G, 16)
+    s_G1, s_G2 = sem(), sem()
+    S.wait_ge(T.sem.arr1, NR * HUB_ENGINES)
+    S.dma_start(T.G1[0:NR, :], T.gd1[:]).then_inc(s_G1, 16)
+    A.wait_ge(T.sem.arr2, NR * HUB_ENGINES)
+    A.dma_start(T.G2[0:NR, :], T.gd2[:]).then_inc(s_G2, 16)
 
-    W = 128 * NSTAT
+    W = 128 * NS2
     s_tm, s_tM, s_tA, s_tC = sem(), sem(), sem(), sem()
     P.wait_ge(s_k11, 1)
-    P.wait_ge(s_G, 16)
-    P.matmul(T.tm_ps[:, 0:NR + 1], T.G[0:NR, 0:W:NSTAT], T.k11[0:NR, 0:NR + 1], True, True).then_inc(s_tm, 1)
-    P.matmul(T.tM_ps[:, 0:1], T.G[0:NR, 2:W:NSTAT], T.k11[0:NR, NR:NR + 1], True, True).then_inc(s_tM, 1)
-    P.matmul(T.tA_ps[:, 0:NR + 1], T.G[0:NR, 1:W:NSTAT], T.k11[0:NR, 0:NR + 1], True, True).then_inc(s_tA, 1)
-    P.matmul(T.tC_ps[:, 0:1], T.G[0:NR, 3:W:NSTAT], T.k11[0:NR, NR:NR + 1], True, True).then_inc(s_tC, 1)
+    P.wait_ge(s_G1, 16)
+    P.matmul(T.tm_ps[:, 0:NR + 1], T.G1[0:NR, :], T.k11[0:NR, 0:NR + 1], True, True).then_inc(s_tm, 1)
+    P.wait_ge(s_G2, 16)
+    P.matmul(T.tM_ps[:, 0:1], T.G2[0:NR, 1:W:NS2], T.k11[0:NR, NR:NR + 1], True, True).then_inc(s_tM, 1)
+    P.matmul(T.tA_ps[:, 0:NR + 1], T.G2[0:NR, 0:W:NS2], T.k11[0:NR, 0:NR + 1], True, True).then_inc(s_tA, 1)
+    P.matmul(T.tC_ps[:, 0:1], T.G2[0:NR, 2:W:NS2], T.k11[0:NR, NR:NR + 1], True, True).then_inc(s_tC, 1)
 
     s_pm, s_v1, s_nm, s_ssd, s_v = sem(), sem(), sem(), sem(), sem()
     V.wait_ge(s_tm, 1)
     V.tensor_scalar(POSMU, T.tm_ps[:, NR:NR + 1], -1.0 / NR, None, MUL).then_inc(s_pm, 1)
     A.wait_ge(s_pm, 1)
     A.activation(T.j10[:, 0:NR], T.tm_ps[:, 0:NR], F.Square, bias=POSMU, accum_out=SSD).then_inc(s_ssd, 1)
-    V.wait_ge(s_tM, 1)
-    V.tensor_scalar(V1, T.tM_ps[:, 0:1], 1.0 / D, EPS, MUL, ADD).then_inc(s_v1, 1)
     V.wait_ge(s_pm, 1)
     V.tensor_scalar(NEGMU, POSMU, -1.0, None, MUL).then_inc(s_nm, 1)
+    V.wait_ge(s_tM, 1)
+    V.tensor_scalar(V1, T.tM_ps[:, 0:1], 1.0 / D, EPS, MUL, ADD).then_inc(s_v1, 1)
     V.wait_ge(s_ssd, 1)
     V.wait_ge(s_v1, 1)
     V.tensor_scalar(VV, SSD, 128.0 / D, V1, MUL, ADD).then_inc(s_v, 1)
@@ -261,4 +290,4 @@ def rank_program(g, core, T, topo):
     S.wait_ge(s_o, 1)
     S.dma_start(T.dx[:], T.dx_sb[:]).then_inc(s_st, 16)
     S.wait_ge(s_st, 16)
-    g.wait_ge(T.sem.lsem, HOP1_ENGINES * len(trs))
+    g.wait_ge(T.sem.lsem, 2 * HOP1_ENGINES * len(ways))

from concourse.bass import DstId, RemoteDMATransfer
from concourse.mybir import AluOpType, AxisListType, ActivationFunctionType

NR = 10
TK = 128
D = 128 * NR
EPS = 0.01
NS2 = 3
HOP1_ENGINES = 4
HUB_ENGINES = 1

SCRATCH = {
    "x_sb": ("sbuf", [128, 128], "float32"),
    "dy_sb": ("sbuf", [128, 128], "float32"),
    "ident": ("sbuf", [128, 128], "float32"),
    "onec": ("sbuf", [128, 4], "float32"),
    "k11": ("sbuf", [128, 12], "float32"),
    "xT": ("sbuf", [128, 128], "float32"),
    "dyT": ("sbuf", [128, 128], "float32"),
    "xc": ("sbuf", [128, 128], "float32"),
    "pr": ("sbuf", [128, 128], "float32"),
    "junk": ("sbuf", [128, 128], "float32"),
    "stat1": ("sbuf", [128, 1], "float32"),
    "stat2": ("sbuf", [128, NS2], "float32"),
    "col": ("sbuf", [128, 16], "float32"),
    "G1": ("sbuf", [128, 128], "float32"),
    "G2": ("sbuf", [128, 128 * NS2], "float32"),
    "j10": ("sbuf", [128, 12], "float32"),
    "dl": ("sbuf", [128, 12], "float32"),
    "dA": ("sbuf", [128, 12], "float32"),
    "w": ("sbuf", [128, 128], "float32"),
    "u": ("sbuf", [128, 128], "float32"),
    "t3": ("sbuf", [128, 128], "float32"),
    "dsd": ("sbuf", [128, 128], "float32"),
    "dx_sb": ("sbuf", [128, 128], "float32"),
    "hub1": ("dram", [3, 128, 1], "float32"),
    "hub2": ("dram", [3, 128, NS2], "float32"),
    "gd1": ("dram", [NR, 128, 1], "float32"),
    "gd2": ("dram", [NR, 128, NS2], "float32"),
    "s1_ps": ("psum", [128, 512], "float32"),
    "xT_ps": ("psum", [128, 512], "float32"),
    "dyT_ps": ("psum", [128, 512], "float32"),
    "tm_ps": ("psum", [128, 512], "float32"),
    "tM_ps": ("psum", [128, 512], "float32"),
    "tA_ps": ("psum", [128, 512], "float32"),
    "tC_ps": ("psum", [128, 512], "float32"),
    "dx_ps": ("psum", [128, 512], "float32"),
}
NSEM = 48
SEMAPHORES = ["harr1", "harr2", "arr1", "arr2", "lsem"] + ["s%d" % k for k in range(NSEM)]

_CACHE = {}


def _plan(T, topo):
    if "hubs" in _CACHE:
        return _CACHE["hubs"]
    ranks = list(T.cores)
    hosts = sorted({topo.host(c) for c in ranks})
    kinds = [[c] for c in ranks]
    merged = True
    while merged:
        merged = False
        for i in range(len(kinds)):
            for j in range(i + 1, len(kinds)):
                if any(topo.may_write(a, b) and topo.may_write(b, a) for a in kinds[i] for b in kinds[j]):
                    kinds[i] = kinds[i] + kinds[j]
                    del kinds[j]
                    merged = True
                    break
            if merged:
                break

    def cabled(h):
        for h2 in hosts:
            if topo.rack(h2) != topo.rack(h) and any(
                    topo.may_write(a, b) for a in ranks if topo.host(a) == h for b in ranks if topo.host(b) == h2):
                return h2
        return None

    hubs = []
    for kind in kinds:
        for h in hosts:
            here = [c for c in kind if topo.host(c) == h]
            srcs = here + [c for c in kind if topo.host(c) == cabled(h)]
            dsts = [c for c in ranks if topo.rack(topo.host(c)) == topo.rack(h)]
            cand = [c for c in range(max(ranks) + 128)
                    if topo.host(c) == h and topo.chip(c) == topo.chip(here[0]) and c not in ranks
                    and topo.die(c) == topo.die(here[0])
                    and all(topo.may_write(c, d) for d in dsts) and all(topo.may_write(s, c) for s in srcs)]
            hubs.append((cand[0], srcs, dsts))
    for d in ranks:
        got = sorted(s for (_, srcs, dsts) in hubs if d in dsts for s in srcs)
        assert got == sorted(ranks)
    _CACHE["hubs"] = hubs
    return hubs


def _engines(topo, src, dsts):
    m = topo.mask(src, dsts[0])
    for d in dsts[1:]:
        m &= topo.mask(src, d)
    return [e for e in range(16) if (m >> e) & 1]


def _spread(es):
    return es[0::2] + es[1::2]


def _bits(es):
    m = 0
    for e in es:
        m |= 1 << e
    return m


def _dst(topo, d, src):
    rid, pid = topo.addr(d, src)
    return DstId(rid=rid, pnc=pid)


def _hub_program(g, core, T, topo, srcs, dsts):
    es = _spread(_engines(topo, core, dsts))
    k = HUB_ENGINES
    for (landed, slots, out, arrived) in ((T.sem.harr1, T.hub1, T.gd1, T.sem.arr1),
                                          (T.sem.harr2, T.hub2, T.gd2, T.sem.arr2)):
        g.wait_ge(landed, HOP1_ENGINES * len(srcs))
        trs = []
        for i, s in enumerate(srcs):
            r = T.rank_of(s)
            trs.append(RemoteDMATransfer(dst_ids=[_dst(topo, d, core) for d in dsts],
                                         dma_engine_mask=_bits(es[i * k:(i + 1) * k]),
                                         remote_sem=arrived, srcs=[slots[i]], dsts=[out[r] for _ in dsts]))
        g.remote_dma_fused(trs, local_sem=T.sem.lsem)
    g.wait_ge(T.sem.lsem, 2 * k * len(srcs))


def rank_program(g, core, T, topo):
    hubs = _plan(T, topo)
    for (h, srcs, dsts) in hubs:
        if h == core:
            _hub_program(g, core, T, topo, srcs, dsts)
            return
    if T.rank_of(core) is None:
        return

    V, A, P, S = g.vector, g.scalar, g.tensor, g.sync
    MUL, ADD, SUB = AluOpType.mult, AluOpType.add, AluOpType.subtract
    F = ActivationFunctionType
    n = [0]

    def sem():
        n[0] += 1
        return T.sem["s%d" % (n[0] - 1)]

    def col(k):
        return T.col[:, k:k + 1]

    POSMU, NEGMU, V1, SSD, VV, RV, RVD, NEGA, SDA, CS, Q2 = [col(k) for k in range(11)]
    M_R = T.stat1[:, 0:1]

    s_x, s_dy = sem(), sem()
    S.dma_start(T.x_sb[:], T.x[:]).then_inc(s_x, 16)
    A.dma_start(T.dy_sb[:], T.dy[:]).then_inc(s_dy, 16)
    s_oc, s_one, s_k1, s_id, s_k11 = sem(), sem(), sem(), sem(), sem()
    V.memset(T.onec[:, 0:1], 1.0).then_inc(s_oc, 1)
    V.memset(T.ident[:], 1.0).then_inc(s_one, 1)
    V.memset(T.k11[0:NR, 0:NR + 1], 1.0).then_inc(s_k1, 1)
    g.wait_ge(s_one, 1)
    g.affine_select(T.ident[:], T.ident[:], [[-1, 128]], AluOpType.is_equal, 0.0, 0, 1).then_inc(s_id, 1)
    g.wait_ge(s_k1, 1)
    g.affine_select(T.k11[0:NR, 0:NR], T.k11[0:NR, 0:NR], [[-1, NR]], AluOpType.is_equal, 0.0, 0, 1).then_inc(s_k11, 1)

    s_s1, s_xT, s_dyT = sem(), sem(), sem()
    P.wait_ge(s_oc, 1)
    P.wait_ge(s_x, 16)
    P.matmul(T.s1_ps[:, 0:1], T.x_sb[:], T.onec[:, 0:1], True, True).then_inc(s_s1, 1)
    P.wait_ge(s_id, 1)
    P.transpose(T.xT_ps[:, 0:128], T.x_sb[:], T.ident[:]).then_inc(s_xT, 1)
    P.wait_ge(s_dy, 16)
    P.transpose(T.dyT_ps[:, 0:128], T.dy_sb[:], T.ident[:]).then_inc(s_dyT, 1)

    s_m, s_xs, s_xc, s_pr, s_c, s_M, s_A = sem(), sem(), sem(), sem(), sem(), sem(), sem()
    V.wait_ge(s_s1, 1)
    V.tensor_scalar(M_R, T.s1_ps[:, 0:1], -1.0 / 128.0, None, MUL).then_inc(s_m, 1)
    A.wait_ge(s_xT, 1)
    A.activation(T.xT[:], T.xT_ps[:, 0:128], F.Identity).then_inc(s_xs, 1)
    V.wait_ge(s_m, 1)
    V.wait_ge(s_xs, 1)
    V.tensor_scalar(T.xc[:], T.xT[:], M_R, None, ADD).then_inc(s_xc, 1)
    A.wait_ge(s_m, 1)
    A.wait_ge(s_xs, 1)
    A.activation(T.junk[:], T.xT[:], F.Square, bias=M_R, accum_out=T.stat2[:, 1:2]).then_inc(s_M, 1)
    V.wait_ge(s_xc, 1)
    V.wait_ge(s_dyT, 1)
    V.tensor_tensor(T.pr[:], T.dyT_ps[:, 0:128], T.xc[:], MUL).then_inc(s_pr, 1)
    V.wait_ge(s_pr, 1)
    V.tensor_reduce(T.stat2[:, 2:3], T.pr[:], AxisListType.X, ADD).then_inc(s_c, 1)
    A.wait_ge(s_pr, 1)
    A.activation(T.dyT[:], T.dyT_ps[:, 0:128], F.Identity, accum_out=T.stat2[:, 0:1]).then_inc(s_A, 1)

    mine = [(h, srcs.index(core)) for (h, srcs, _) in hubs if core in srcs]
    far = [e for (h, _) in mine for e in _engines(topo, core, [h])]
    narrow = [e for e in range(16) if far.count(e) == len(mine)]
    used, ways = [], []
    for (h, slot) in sorted(mine, key=lambda t: len(_engines(topo, core, [t[0]]))):
        es = _engines(topo, core, [h])
        wide = [e for e in es if e not in narrow and e not in used]
        pick = _spread(wide if len(wide) >= HOP1_ENGINES else [e for e in es if e not in used])[0:HOP1_ENGINES]
        used += pick
        ways.append((h, slot, _bits(pick)))
    g.wait_ge(s_m, 1)
    g.remote_dma_fused([RemoteDMATransfer(dst_ids=[_dst(topo, h, core)], dma_engine_mask=m, remote_sem=T.sem.harr1,
                                          srcs=[T.stat1[:]], dsts=[T.hub1[slot]]) for (h, slot, m) in ways],
                       local_sem=T.sem.lsem)
    for s in (s_A, s_M, s_c):
        g.wait_ge(s, 1)
    g.remote_dma_fused([RemoteDMATransfer(dst_ids=[_dst(topo, h, core)], dma_engine_mask=m, remote_sem=T.sem.harr2,
                                          srcs=[T.stat2[:]], dsts=[T.hub2[slot]]) for (h, slot, m) in ways],
                       local_sem=T.sem.lsem)

    s_G1, s_G2 = sem(), sem()
    S.wait_ge(T.sem.arr1, NR * HUB_ENGINES)
    S.dma_start(T.G1[0:NR, :], T.gd1[:]).then_inc(s_G1, 16)
    A.wait_ge(T.sem.arr2, NR * HUB_ENGINES)
    A.dma_start(T.G2[0:NR, :], T.gd2[:]).then_inc(s_G2, 16)

    W = 128 * NS2
    s_tm, s_tM, s_tA, s_tC = sem(), sem(), sem(), sem()
    P.wait_ge(s_k11, 1)
    P.wait_ge(s_G1, 16)
    P.matmul(T.tm_ps[:, 0:NR + 1], T.G1[0:NR, :], T.k11[0:NR, 0:NR + 1], True, True).then_inc(s_tm, 1)
    P.wait_ge(s_G2, 16)
    P.matmul(T.tM_ps[:, 0:1], T.G2[0:NR, 1:W:NS2], T.k11[0:NR, NR:NR + 1], True, True).then_inc(s_tM, 1)
    P.matmul(T.tA_ps[:, 0:NR + 1], T.G2[0:NR, 0:W:NS2], T.k11[0:NR, 0:NR + 1], True, True).then_inc(s_tA, 1)
    P.matmul(T.tC_ps[:, 0:1], T.G2[0:NR, 2:W:NS2], T.k11[0:NR, NR:NR + 1], True, True).then_inc(s_tC, 1)

    s_pm, s_v1, s_nm, s_ssd, s_v = sem(), sem(), sem(), sem(), sem()
    V.wait_ge(s_tm, 1)
    V.tensor_scalar(POSMU, T.tm_ps[:, NR:NR + 1], -1.0 / NR, None, MUL).then_inc(s_pm, 1)
    A.wait_ge(s_pm, 1)
    A.activation(T.j10[:, 0:NR], T.tm_ps[:, 0:NR], F.Square, bias=POSMU, accum_out=SSD).then_inc(s_ssd, 1)
    V.wait_ge(s_pm, 1)
    V.tensor_scalar(NEGMU, POSMU, -1.0, None, MUL).then_inc(s_nm, 1)
    V.wait_ge(s_tM, 1)
    V.tensor_scalar(V1, T.tM_ps[:, 0:1], 1.0 / D, EPS, MUL, ADD).then_inc(s_v1, 1)
    V.wait_ge(s_ssd, 1)
    V.wait_ge(s_v1, 1)
    V.tensor_scalar(VV, SSD, 128.0 / D, V1, MUL, ADD).then_inc(s_v, 1)

    s_dsd = sem()
    A.wait_ge(s_v, 1)
    A.wait_ge(s_id, 1)
    A.activation(T.dsd[:], T.ident[:], F.Sqrt, scale=VV).then_inc(s_dsd, 1)

    s_rv, s_dl, s_dA, s_na, s_sdA, s_rvD, s_w, s_Cs, s_q2, s_u, s_t3 = [sem() for _ in range(11)]
    V.wait_ge(s_v, 1)
    V.reciprocal(RV, VV).then_inc(s_rv, 1)
    V.tensor_scalar(T.dl[:, 0:NR], T.tm_ps[:, 0:NR], POSMU, None, ADD).then_inc(s_dl, 1)
    V.wait_ge(s_tA, 1)
    V.tensor_scalar(NEGA, T.tA_ps[:, NR:NR + 1], -1.0 / D, None, MUL).then_inc(s_na, 1)
    V.wait_ge(s_dl, 1)
    V.tensor_tensor(T.dA[:, 0:NR], T.dl[:, 0:NR], T.tA_ps[:, 0:NR], MUL).then_inc(s_dA, 1)
    V.wait_ge(s_dA, 1)
    V.tensor_reduce(SDA, T.dA[:, 0:NR], AxisListType.X, ADD).then_inc(s_sdA, 1)
    V.wait_ge(s_rv, 1)
    V.tensor_scalar(RVD, RV, 1.0 / D, None, MUL).then_inc(s_rvD, 1)
    V.wait_ge(s_sdA, 1)
    V.wait_ge(s_tC, 1)
    V.tensor_scalar(CS, T.tC_ps[:, 0:1], SDA, None, SUB).then_inc(s_Cs, 1)
    V.wait_ge(s_Cs, 1)
    V.wait_ge(s_rvD, 1)
    V.tensor_scalar(Q2, CS, RV, RVD, MUL, MUL).then_inc(s_q2, 1)
    V.wait_ge(s_na, 1)
    V.wait_ge(s_A, 1)
    V.tensor_scalar(T.w[:], T.dyT[:], NEGA, RV, ADD, MUL).then_inc(s_w, 1)
    V.wait_ge(s_q2, 1)
    V.wait_ge(s_nm, 1)
    V.tensor_scalar(T.u[:], T.xT[:], NEGMU, Q2, ADD, MUL).then_inc(s_u, 1)
    V.wait_ge(s_u, 1)
    V.wait_ge(s_w, 1)
    V.tensor_tensor(T.t3[:], T.w[:], T.u[:], SUB).then_inc(s_t3, 1)

    s_dx, s_o, s_st = sem(), sem(), sem()
    P.wait_ge(s_t3, 1)
    P.wait_ge(s_dsd, 1)
    P.matmul(T.dx_ps[:, 0:128], T.t3[:], T.dsd[:], True, True).then_inc(s_dx, 1)
    V.wait_ge(s_dx, 1)
    V.tensor_copy(T.dx_sb[:], T.dx_ps[:, 0:128]).then_inc(s_o, 1)
    S.wait_ge(s_o, 1)
    S.dma_start(T.dx[:], T.dx_sb[:]).then_inc(s_st, 16)
    S.wait_ge(s_st, 16)
    g.wait_ge(T.sem.lsem, 2 * HOP1_ENGINES * len(ways))
